import numpy as np
import ml_dtypes


def mxq(x, axis, fmt="e4m3"):
    dtype, down = {"e4m3": (ml_dtypes.float8_e4m3fn, 7), "e5m2": (ml_dtypes.float8_e5m2, 14)}[fmt]
    v = np.moveaxis(np.asarray(x, np.float32).astype(ml_dtypes.bfloat16).astype(np.float64), axis, -1)
    blocks = v.reshape(v.shape[:-1] + (-1, 32))
    amax = np.abs(blocks).max(-1, keepdims=True)
    byte = np.maximum(np.where(amax > 0, np.frexp(amax)[1] - 1 + 127, 0) - down, 1)
    scale = np.exp2(byte - 127.0)
    codes = (blocks / scale).astype(np.float32).astype(dtype).astype(np.float64)
    return np.moveaxis((codes * scale).reshape(v.shape), -1, axis)


WIDE = False


def mx_kscale(k):
    if not WIDE:
        return np.ones(k)
    levels = np.array([10, -10, 5, -5, 0])
    if k % 512:
        return np.exp2(np.random.permutation(np.resize(levels, k // 32))).repeat(32)
    a = np.empty((k // 512, 16))
    for p in range(k // 512):
        a[p, :8] = np.random.permutation(np.resize(levels, 8))
        for g in range(8):
            far = levels[np.abs(levels - a[p, g]) >= 10]
            a[p, g + 8] = far[np.random.randint(len(far))]
    return np.exp2(a.ravel()).repeat(32)


def f64(x):
    return np.asarray(x).astype(np.float64)


def striped(idx):
    return np.tile(idx.reshape(-1, 16).T, (8, 1)).astype(np.uint16)


def unstriped(offs):
    return offs[:16].T.reshape(-1).astype(np.int64)


E2M1 = np.array([0.0, 0.5, 1.0, 1.5, 2.0, 3.0, 4.0, 6.0, -0.0, -0.5, -1.0, -1.5, -2.0, -3.0, -4.0, -6.0])


def pack_weight(w, fmt):
    k, n = w.shape
    w = f64(np.asarray(w, np.float32).astype(ml_dtypes.bfloat16)).reshape(k // 32, 32, n)
    amax = np.abs(w).max(1)
    if fmt == "e4m3":
        byte = np.frexp(amax)[1] - 1 + 127 - 7
    else:
        mant, ex = np.frexp(amax / 6.0)
        byte = np.where(mant > 0.5, ex, ex - 1) + 127
    byte = np.clip(np.where(amax > 0, byte, 1), 1, 254)
    scaled = (w * np.exp2(127.0 - byte)[:, None, :]).reshape(k, n).astype(np.float32)
    by_word = np.ascontiguousarray(scaled.reshape(k // 512, 128, 4, n).transpose(0, 1, 3, 2))
    if fmt == "e4m3":
        words = by_word.astype(ml_dtypes.float8_e4m3fn).view(np.uint8)
    else:
        c = by_word.astype(ml_dtypes.float4_e2m1fn).view(np.uint8) & 0xF
        words = (c[..., 0::2] | (c[..., 1::2] << 4)).reshape(k // 512, 128, 2 * n)
    return np.ascontiguousarray(words), np.ascontiguousarray(byte.astype(np.uint8).reshape(k // 512, 16, n))


def unpack_weight(words, scales, fmt):
    g, _, n = scales.shape
    words = np.ascontiguousarray(words).reshape(g, 128, n, -1)
    if fmt == "e4m3":
        vals = words.view(ml_dtypes.float8_e4m3fn).astype(np.float64)
    else:
        nib = np.empty((g, 128, n, 4), np.uint8)
        nib[..., 0::2] = words & 0xF
        nib[..., 1::2] = words >> 4
        vals = E2M1[nib]
    vals = vals * np.repeat(np.exp2(scales.astype(np.float64) - 127.0), 8, axis=1)[..., None]
    return vals.transpose(0, 1, 3, 2).reshape(g * 512, n)


def gelu(v):
    return 0.5 * v * (1.0 + np.tanh(np.sqrt(2.0 / np.pi) * (v + 0.044715 * v**3)))


K, T, S, H, P, N = 1536, 2048, 1024, 512, 512, 768

def setup_inputs():
    n = np.random.standard_normal
    s = mx_kscale(K)[:, None]
    u = mx_kscale(H)[:, None]
    d = {}
    d["tab_words"], d["tab_scales"] = pack_weight(n((K, T)) * s, "e2m1")
    d["offs"] = striped(np.random.permutation(T)[:S])
    d["pos1"] = striped(np.random.permutation(S)[:P])
    d["pos2"] = striped(np.random.permutation(S)[:P])
    d["w1"] = (0.40 * n((K, H)) / K**0.5 / s).astype(np.float32)
    d["w2_words"], d["w2_scales"] = pack_weight(0.36 * n((K, H)) / K**0.5 / s, "e4m3")
    d["b1"] = np.random.uniform(-0.3, 1.0, H).astype(np.float32)
    d["gain"] = (np.exp(0.3 * n(H)) * u[:, 0]).astype(np.float32)
    d["w4_words"], d["w4_scales"] = pack_weight(1.3 * n((H, N)) / H**0.5 / u, "e2m1")
    d["caps"] = (0.3 + 0.8 * n((N, P))).astype(np.float32)
    return d

def reference(tab_words, tab_scales, offs, pos1, pos2, w1, w2_words, w2_scales, b1, gain,
              w4_words, w4_scales, caps):
    v = unpack_weight(tab_words, tab_scales, "e2m1")[:, unstriped(offs)]
    lift = mxq(f64(w1), 0, "e4m3").T @ v
    warp = unpack_weight(w2_words, w2_scales, "e4m3").T @ v
    h = lift + f64(b1)[:, None] - np.abs(warp)
    upper = h[:, unstriped(pos1)]
    lower = h[:, unstriped(pos2)]
    z = (upper + np.sin(lower)) * f64(gain)[:, None]
    w4 = unpack_weight(w4_words, w4_scales, "e2m1")
    y = w4.T @ mxq(z, 0, "e4m3")
    return np.minimum(y, f64(caps))

@@ -1,0 +1,263 @@
+from contextlib import ExitStack
+
+import concourse.mybir as mybir
+
+K, T, S, H, PAIRS, N = 1536, 2048, 1024, 512, 512, 768
+FLOPS = 2 * (2 * K * H * S + H * N * PAIRS)
+
+F32 = mybir.dt.float32
+BF16 = mybir.dt.bfloat16
+I32 = mybir.dt.int32
+U32 = mybir.dt.uint32
+U16 = mybir.dt.uint16
+U8 = mybir.dt.uint8
+FP8X4 = mybir.dt.float8_e4m3fn_x4
+FP4X4 = mybir.dt.float4_e2m1fn_x4
+ACT = mybir.ActivationFunctionType
+ALU = mybir.AluOpType
+
+P = 128
+PACK = 4
+PASSES = K // (P * PACK)
+HALF_S = S // 2
+HALF_J = PAIRS // 2
+HALF_C = H // 2
+N_TILES = N // P
+ALIGN = 64
+
+
+def tile_list_cane_blade_pairing_kernel(
+    tc, tab_words, tab_scales, offs, pos1, pos2, w1, w2_words, w2_scales, b1, gain, w4_words, w4_scales, caps, out
+):
+    nc = tc.nc
+    with ExitStack() as ctx:
+        keep = ctx.enter_context(tc.tile_pool(name="keep", bufs=1))
+        psum = ctx.enter_context(tc.psum_pool(name="psum", bufs=1))
+
+        def sb(shape, dtype, name, tag=""):
+            return keep.tile(shape, dtype, name=name, tag=tag or name, align_bytes=ALIGN)
+
+        tab_sc = sb([P, T], U8, "tab_sc")
+        w2_sc_raw = sb([P, PASSES * H], U8, "w2_sc_raw")
+        w4_sc = sb([P, N], U8, "w4_sc")
+        warm = sb([P, 2], F32, "warm")
+        nc.gpsimd.memset(tab_sc[:].bitcast(I32), 0)
+        nc.vector.memset(w2_sc_raw[:].bitcast(I32), 0)
+        nc.vector.memset(w4_sc[:].bitcast(I32), 0)
+        nc.vector.memset(warm[:, 0:1], 0.0)
+        warm_out = sb([P, 1], F32, "warm_out")
+        nc.scalar.activation(out=warm_out[:], in_=warm[:, 0:1], func=ACT.Sin)
+
+        offs_t = keep.tile([P, S // 16], U16, name="offs_t")
+        pos1_t = keep.tile([P, PAIRS // 16], U16, name="pos1_t")
+        pos2_t = keep.tile([P, PAIRS // 16], U16, name="pos2_t")
+        tab_w = [sb([P, T], U16, "tab_w%d" % a) for a in range(PASSES)]
+        w1_raw = [[sb([P, PACK, HALF_C], F32, "w1_raw%d%d" % (a, c)) for c in range(2)] for a in range(PASSES)]
+        w2_raw = [sb([P, H], I32, "w2_raw%d" % a) for a in range(PASSES)]
+
+        def load_tab(a):
+            nc.sync.dma_start(out=tab_w[a][:].bitcast(I32), in_=tab_words[a].bitcast(I32))
+
+        def load_w1(a, c):
+            rows = w1[a * P * PACK : (a + 1) * P * PACK, c * HALF_C : (c + 1) * HALF_C]
+            nc.sync.dma_start(out=w1_raw[a][c][:], in_=rows.rearrange("(p j) c -> p j c", j=PACK))
+
+        def load_w2(a):
+            nc.sync.dma_start(out=w2_raw[a][:], in_=w2_words[a].rearrange("p c i -> p (c i)").bitcast(I32))
+
+        nc.sync.dma_start(offs_t[:], offs)
+        load_tab(0)
+        tab_sc_words = tab_sc[:].bitcast(I32)
+        scale_rows = tab_scales.bitcast(I32).rearrange("a (u e r) t -> e (a u) r t", u=2, e=2)
+        for e in range(2):
+            nc.sync.dma_start(out=tab_sc_words[32 * e + 4 : 32 * e + 20, :], in_=scale_rows[e, 2:6])
+        for u in range(2):
+            for e in range(2):
+                q = 2 * u + e
+                nc.sync.dma_start(out=tab_sc_words[32 * q : 32 * q + 4, :], in_=scale_rows[e, u])
+        v_w = [[sb([P, HALF_S], U16, "v_w%d%d" % (a, s)) for s in range(2)] for a in range(PASSES)]
+        v_sc = [sb([P, S], U8, "v_sc%d" % a) for a in range(PASSES)]
+        w1_bf = [sb([P, H * PACK], BF16, "w1_bf%d" % a) for a in range(PASSES)]
+        w1_q = [sb([P, H], U32, "w1_q%d" % a) for a in range(PASSES)]
+        w1_sc = [sb([P, H], U8, "w1_sc%d" % a) for a in range(PASSES)]
+        w2_q = [sb([P, H], I32, "w2_q%d" % a) for a in range(PASSES)]
+        w2_sc = sb([P, PASSES * H], U8, "w2_sc")
+
+        def gather_words(a):
+            for s in range(2):
+                cols = offs_t[:, s * (HALF_S // 16) : (s + 1) * (HALF_S // 16)]
+                nc.vector.tensor_copy(out=v_w[a][s][:], in_=tab_w[a][:].indirect(cols))
+
+        def cast_w1(a, c):
+            dst = w1_bf[a][:].rearrange("p (t m j) -> p m t j", t=PACK, j=PACK)
+            m_count = HALF_C // PACK
+            nc.scalar.copy(
+                out=dst[:, c * m_count : (c + 1) * m_count],
+                in_=w1_raw[a][c][:].rearrange("p j (m t) -> p m t j", t=PACK),
+            )
+
+        def quantize_w1(a):
+            nc.vector.quantize_mx(out=w1_q[a][:].bitcast(FP8X4), scales=w1_sc[a][:], in_=w1_bf[a][:])
+
+        def deal_w2(a):
+            nc.vector.tensor_copy(
+                out=w2_q[a][:].rearrange("p (t g i) -> p g t i", t=PACK, i=4),
+                in_=w2_raw[a][:].rearrange("p (g i t) -> p g t i", t=PACK, i=4),
+            )
+
+        gather_words(0)
+        nc.vector.tensor_copy(out=v_sc[0][:], in_=tab_sc[:].indirect(offs_t[:]))
+        for a in range(1, PASSES):
+            for u in range(2):
+                first = 4 * (2 * a + u - 1)
+                nc.sync.dma_start(
+                    out=v_sc[a][:].bitcast(I32)[64 * u : 64 * u + 64, :],
+                    in_=v_sc[0][:].bitcast(I32)[first : first + 64, :],
+                )
+        load_w1(0, 0)
+        load_w1(0, 1)
+        load_tab(1)
+        w2_sc_words = w2_sc_raw[:].bitcast(I32).rearrange("p (a c) -> p a c", a=PASSES)
+        w2_sc_rows = w2_scales.bitcast(I32).rearrange("a r c -> r a c")
+        for q in range(4):
+            nc.sync.dma_start(out=w2_sc_words[32 * q : 32 * q + 4], in_=w2_sc_rows[4 * q : 4 * q + 4])
+        for a in range(PASSES):
+            load_w2(a)
+        for a in range(1, PASSES):
+            load_w1(a, 0)
+            load_w1(a, 1)
+        load_tab(2)
+        nc.sync.dma_start(pos2_t[:], pos2)
+        nc.sync.dma_start(pos1_t[:], pos1)
+
+        b1_t = sb([P, PACK], F32, "b1_t")
+        gain_t = sb([P, PACK], F32, "gain_t")
+        nc.sync.dma_start(out=b1_t[:], in_=b1.rearrange("(p t) -> p t", t=PACK))
+        nc.sync.dma_start(out=gain_t[:], in_=gain.rearrange("(p t) -> p t", t=PACK))
+
+        for q in range(4):
+            nc.sync.dma_start(
+                out=w4_sc[:].bitcast(I32)[32 * q : 32 * q + 4, :], in_=w4_scales[0].bitcast(I32)[4 * q : 4 * q + 4, :]
+            )
+        for a in range(PASSES):
+            cast_w1(a, 0)
+            cast_w1(a, 1)
+        gather_words(1)
+        quantize_w1(0)
+        nc.vector.tensor_copy(
+            out=w2_sc[:].rearrange("p (a t m) -> p a t m", a=PASSES, t=PACK),
+            in_=w2_sc_raw[:].rearrange("p (a m t) -> p a t m", a=PASSES, t=PACK),
+        )
+        for a in range(PASSES):
+            deal_w2(a)
+        quantize_w1(1)
+        quantize_w1(2)
+        gather_words(2)
+
+        w4_w = sb([P, 2 * N], U8, "w4_w")
+        nc.sync.dma_start(out=w4_w[:].bitcast(I32), in_=w4_words[0].bitcast(I32))
+        spent = ["w1_raw11", "w1_raw20", "w1_raw21"]
+        caps_t = [sb([P, 2, PAIRS], F32, "caps%d" % i, tag=spent[i]) for i in range(N_TILES // 2)]
+        for i in range(N_TILES // 2):
+            nc.sync.dma_start(
+                out=caps_t[i][:], in_=caps[2 * i * P : 2 * (i + 1) * P, :].rearrange("(u p) j -> p u j", p=P)
+            )
+
+        z_bf = [sb([P, HALF_J * PACK], BF16, "z_bf%d" % g) for g in range(2)]
+        h = [sb([P, S], F32, "h%d" % t) for t in range(PACK)]
+        sines = {}
+
+        def product(t, s, kind, codes, scale_of):
+            bank = psum.tile([P, HALF_S], F32, name="bank", tag="bank%d" % (4 * (t % 2) + 2 * s + kind))
+            for a in range(PASSES):
+                nc.tensor.matmul_mx(
+                    out=bank[:],
+                    lhsT=codes[a][:, t * P : (t + 1) * P].bitcast(FP8X4),
+                    lhsT_scale=scale_of(a),
+                    rhs=v_w[a][s][:].bitcast(FP4X4),
+                    rhs_scale=v_sc[a][:, s * HALF_S : (s + 1) * HALF_S],
+                    start=(a == 0),
+                    stop=(a == PASSES - 1),
+                )
+            return bank
+
+        def first_stage(t):
+            for s in range(2):
+                warp = product(t, s, 0, w2_q, lambda a: w2_sc[:, a * H + t * P : a * H + (t + 1) * P])
+                lift = product(t, s, 1, w1_q, lambda a: w1_sc[a][:, t * P : (t + 1) * P])
+                size = sb([P, HALF_S], F32, "size%d%d" % (t, s))
+                nc.scalar.activation(out=size[:], in_=warp[:], func=ACT.Abs)
+                nc.vector.scalar_tensor_tensor(
+                    out=h[t][:, s * HALF_S : (s + 1) * HALF_S],
+                    in0=lift[:],
+                    scalar=b1_t[:, t : t + 1],
+                    in1=size[:],
+                    op0=ALU.add,
+                    op1=ALU.subtract,
+                )
+
+        def lower_blade(t):
+            lower = sb([P, PAIRS], F32, "lower%d" % t)
+            nc.vector.tensor_copy(out=lower[:], in_=h[t][:].indirect(pos2_t[:]))
+            for g in range(2):
+                sines[t, g] = sb([P, HALF_J], F32, "sine%d%d" % (t, g))
+                nc.scalar.activation(out=sines[t, g][:], in_=lower[:, g * HALF_J : (g + 1) * HALF_J], func=ACT.Sin)
+
+        def upper_blade(t, g, total):
+            cols = pos1_t[:, g * (HALF_J // 16) : (g + 1) * (HALF_J // 16)]
+            nc.vector.tensor_tensor(out=total, in0=h[t][:].indirect(cols), in1=sines[t, g][:], op=ALU.add)
+            nc.scalar.activation(
+                out=z_bf[g][:].rearrange("p (j t) -> p t j", t=PACK)[:, t, :],
+                in_=total,
+                func=ACT.Copy,
+                scale=gain_t[:, t : t + 1],
+            )
+
+        z_q = [sb([P, HALF_J], U32, "z_q%d" % g) for g in range(2)]
+        z_sc = [sb([P, HALF_J], U8, "z_sc%d" % g) for g in range(2)]
+
+        def quantize_z(g):
+            nc.vector.quantize_mx(out=z_q[g][:].bitcast(FP8X4), scales=z_sc[g][:], in_=z_bf[g][:])
+
+        def scores(g):
+            j_cols = slice(g * HALF_J, (g + 1) * HALF_J)
+            for i in range(N_TILES // 2):
+                bank = psum.tile([P, 2 * HALF_J], F32, name="bank", tag="bank%d" % (3 * g + i))
+                for u in range(2):
+                    n0 = (2 * i + u) * P
+                    nc.tensor.matmul_mx(
+                        out=bank[:, u * HALF_J : (u + 1) * HALF_J],
+                        lhsT=w4_w[:, 2 * n0 : 2 * (n0 + P)].bitcast(FP4X4),
+                        lhsT_scale=w4_sc[:, n0 : n0 + P],
+                        rhs=z_q[g][:].bitcast(FP8X4),
+                        rhs_scale=z_sc[g][:],
+                        start=True,
+                        stop=True,
+                    )
+                capped = sb([P, 2, HALF_J], F32, "capped%d%d" % (g, i))
+                nc.vector.tensor_tensor(
+                    out=capped[:],
+                    in0=bank[:].rearrange("p (u j) -> p u j", u=2),
+                    in1=caps_t[i][:, :, j_cols],
+                    op=ALU.min,
+                )
+                nc.sync.dma_start(
+                    out=out[2 * i * P : 2 * (i + 1) * P, j_cols].rearrange("(u p) j -> p u j", p=P), in_=capped[:]
+                )
+
+        last = PACK - 1
+        for t in range(PACK):
+            first_stage(t)
+            lower_blade(t)
+            if t > 0:
+                upper_blade(t - 1, 0, sb([P, HALF_J], F32, "total%d0" % (t - 1), tag="size%d1" % t)[:])
+        upper_blade(0, 1, sb([P, HALF_J], F32, "total01", tag="size%d0" % last)[:])
+        upper_blade(last, 0, sb([P, HALF_J], F32, "total%d0" % last)[:])
+        late = sb([P, last, HALF_J], F32, "late_totals", tag="sine%d0" % last)
+        upper_blade(1, 1, late[:, 0, :])
+        upper_blade(2, 1, late[:, 1, :])
+        quantize_z(0)
+        upper_blade(3, 1, late[:, 2, :])
+        scores(0)
+        quantize_z(1)
+        scores(1)

@@ -75,7 +75,7 @@ def tile_list_cane_blade_pairing_kernel(
             for e in range(2):
                 q = 2 * u + e
                 nc.sync.dma_start(out=tab_sc_words[32 * q : 32 * q + 4, :], in_=scale_rows[e, u])
-        v_w = [[sb([P, HALF_S], U16, "v_w%d%d" % (a, s)) for s in range(2)] for a in range(PASSES)]
+        v_w = {}
         v_sc = [sb([P, S], U8, "v_sc%d" % a) for a in range(PASSES)]
         w1_bf = [sb([P, H * PACK], BF16, "w1_bf%d" % a) for a in range(PASSES)]
         w1_q = [sb([P, H], U32, "w1_q%d" % a) for a in range(PASSES)]
@@ -83,10 +83,10 @@ def tile_list_cane_blade_pairing_kernel(
         w2_q = [sb([P, H], I32, "w2_q%d" % a) for a in range(PASSES)]
         w2_sc = sb([P, PASSES * H], U8, "w2_sc")
 
-        def gather_words(a):
-            for s in range(2):
-                cols = offs_t[:, s * (HALF_S // 16) : (s + 1) * (HALF_S // 16)]
-                nc.vector.tensor_copy(out=v_w[a][s][:], in_=tab_w[a][:].indirect(cols))
+        def gather_words(a, s, tag=""):
+            v_w[a, s] = sb([P, HALF_S], U16, "v_w%d%d" % (a, s), tag=tag)
+            cols = offs_t[:, s * (HALF_S // 16) : (s + 1) * (HALF_S // 16)]
+            nc.vector.tensor_copy(out=v_w[a, s][:], in_=tab_w[a][:].indirect(cols))
 
         def cast_w1(a, c):
             dst = w1_bf[a][:].rearrange("p (t m j) -> p m t j", t=PACK, j=PACK)
@@ -105,12 +105,13 @@ def tile_list_cane_blade_pairing_kernel(
                 in_=w2_raw[a][:].rearrange("p (g i t) -> p g t i", t=PACK, i=4),
             )
 
-        gather_words(0)
+        gather_words(0, 0)
+        gather_words(0, 1)
         nc.vector.tensor_copy(out=v_sc[0][:], in_=tab_sc[:].indirect(offs_t[:]))
         for a in range(1, PASSES):
             for u in range(2):
                 first = 4 * (2 * a + u - 1)
-                nc.sync.dma_start(
+                nc.gpsimd.dma_start(
                     out=v_sc[a][:].bitcast(I32)[64 * u : 64 * u + 64, :],
                     in_=v_sc[0][:].bitcast(I32)[first : first + 64, :],
                 )
@@ -142,7 +143,8 @@ def tile_list_cane_blade_pairing_kernel(
         for a in range(PASSES):
             cast_w1(a, 0)
             cast_w1(a, 1)
-        gather_words(1)
+        gather_words(1, 0)
+        gather_words(1, 1)
         quantize_w1(0)
         nc.vector.tensor_copy(
             out=w2_sc[:].rearrange("p (a t m) -> p a t m", a=PASSES, t=PACK),
@@ -151,8 +153,9 @@ def tile_list_cane_blade_pairing_kernel(
         for a in range(PASSES):
             deal_w2(a)
         quantize_w1(1)
+        gather_words(2, 0)
         quantize_w1(2)
-        gather_words(2)
+        gather_words(2, 1, tag="w1_bf2")
 
         w4_w = sb([P, 2 * N], U8, "w4_w")
         nc.sync.dma_start(out=w4_w[:].bitcast(I32), in_=w4_words[0].bitcast(I32))
@@ -166,6 +169,7 @@ def tile_list_cane_blade_pairing_kernel(
         z_bf = [sb([P, HALF_J * PACK], BF16, "z_bf%d" % g) for g in range(2)]
         h = [sb([P, S], F32, "h%d" % t) for t in range(PACK)]
         sines = {}
+        lowers = {}
 
         def product(t, s, kind, codes, scale_of):
             bank = psum.tile([P, HALF_S], F32, name="bank", tag="bank%d" % (4 * (t % 2) + 2 * s + kind))
@@ -174,7 +178,7 @@ def tile_list_cane_blade_pairing_kernel(
                     out=bank[:],
                     lhsT=codes[a][:, t * P : (t + 1) * P].bitcast(FP8X4),
                     lhsT_scale=scale_of(a),
-                    rhs=v_w[a][s][:].bitcast(FP4X4),
+                    rhs=v_w[a, s][:].bitcast(FP4X4),
                     rhs_scale=v_sc[a][:, s * HALF_S : (s + 1) * HALF_S],
                     start=(a == 0),
                     stop=(a == PASSES - 1),
@@ -199,13 +203,15 @@ def tile_list_cane_blade_pairing_kernel(
         def lower_blade(t):
             lower = sb([P, PAIRS], F32, "lower%d" % t)
             nc.vector.tensor_copy(out=lower[:], in_=h[t][:].indirect(pos2_t[:]))
-            for g in range(2):
-                sines[t, g] = sb([P, HALF_J], F32, "sine%d%d" % (t, g))
-                nc.scalar.activation(out=sines[t, g][:], in_=lower[:, g * HALF_J : (g + 1) * HALF_J], func=ACT.Sin)
+            lowers[t] = lower
+
+        def sine(t, tag=""):
+            sines[t] = sb([P, PAIRS], F32, "sine%d" % t, tag=tag)
+            nc.scalar.activation(out=sines[t][:], in_=lowers[t][:], func=ACT.Sin)
 
         def upper_blade(t, g, total):
             cols = pos1_t[:, g * (HALF_J // 16) : (g + 1) * (HALF_J // 16)]
-            nc.vector.tensor_tensor(out=total, in0=h[t][:].indirect(cols), in1=sines[t, g][:], op=ALU.add)
+            nc.vector.tensor_tensor(out=total, in0=h[t][:].indirect(cols), in1=sines[t][:, g * HALF_J : (g + 1) * HALF_J], op=ALU.add)
             nc.scalar.activation(
                 out=z_bf[g][:].rearrange("p (j t) -> p t j", t=PACK)[:, t, :],
                 in_=total,
@@ -248,16 +254,19 @@ def tile_list_cane_blade_pairing_kernel(
         last = PACK - 1
         for t in range(PACK):
             first_stage(t)
-            lower_blade(t)
             if t > 0:
-                upper_blade(t - 1, 0, sb([P, HALF_J], F32, "total%d0" % (t - 1), tag="size%d1" % t)[:])
-        upper_blade(0, 1, sb([P, HALF_J], F32, "total01", tag="size%d0" % last)[:])
-        upper_blade(last, 0, sb([P, HALF_J], F32, "total%d0" % last)[:])
-        late = sb([P, last, HALF_J], F32, "late_totals", tag="sine%d0" % last)
-        upper_blade(1, 1, late[:, 0, :])
-        upper_blade(2, 1, late[:, 1, :])
+                sine(t - 1, tag="size%d1" % t)
+            lower_blade(t)
+        sine(last)
+        early = sb([P, PACK, HALF_J], F32, "early_totals", tag="lower%d" % (last - 1))
+        for t in range(PACK):
+            upper_blade(t, 0, early[:, t, :])
+        late = sb([P, PACK, HALF_J], F32, "late_totals", tag="lower%d" % last)
+        upper_blade(0, 1, late[:, 0, :])
+        upper_blade(1, 1, late[:, 1, :])
         quantize_z(0)
-        upper_blade(3, 1, late[:, 2, :])
+        upper_blade(2, 1, late[:, 2, :])
+        upper_blade(3, 1, late[:, 3, :])
         scores(0)
         quantize_z(1)
         scores(1)

@@ -53,7 +53,7 @@ def tile_list_cane_blade_pairing_kernel(
         pos2_t = keep.tile([P, PAIRS // 16], U16, name="pos2_t")
         tab_w = [sb([P, T], U16, "tab_w%d" % a) for a in range(PASSES)]
         w1_raw = [[sb([P, PACK, HALF_C], F32, "w1_raw%d%d" % (a, c)) for c in range(2)] for a in range(PASSES)]
-        w2_raw = [sb([P, H], I32, "w2_raw%d" % a) for a in range(PASSES)]
+        w2_raw = sb([P, PASSES, H], I32, "w2_raw")
 
         def load_tab(a):
             nc.sync.dma_start(out=tab_w[a][:].bitcast(I32), in_=tab_words[a].bitcast(I32))
@@ -61,9 +61,6 @@ def tile_list_cane_blade_pairing_kernel(
         def load_w1(a, c):
             rows = w1[a * P * PACK : (a + 1) * P * PACK, c * HALF_C : (c + 1) * HALF_C]
             nc.sync.dma_start(out=w1_raw[a][c][:], in_=rows.rearrange("(p j) c -> p j c", j=PACK))
-
-        def load_w2(a):
-            nc.sync.dma_start(out=w2_raw[a][:], in_=w2_words[a].rearrange("p c i -> p (c i)").bitcast(I32))
 
         nc.sync.dma_start(offs_t[:], offs)
         load_tab(0)
@@ -76,7 +73,7 @@ def tile_list_cane_blade_pairing_kernel(
                 q = 2 * u + e
                 nc.sync.dma_start(out=tab_sc_words[32 * q : 32 * q + 4, :], in_=scale_rows[e, u])
         v_w = {}
-        v_sc = [sb([P, S], U8, "v_sc%d" % a) for a in range(PASSES)]
+        v_sc = [sb([P, S], U8, "v_sc0")]
         w1_bf = [sb([P, H * PACK], BF16, "w1_bf%d" % a) for a in range(PASSES)]
         w1_q = [sb([P, H], U32, "w1_q%d" % a) for a in range(PASSES)]
         w1_sc = [sb([P, H], U8, "w1_sc%d" % a) for a in range(PASSES)]
@@ -88,13 +85,13 @@ def tile_list_cane_blade_pairing_kernel(
             cols = offs_t[:, s * (HALF_S // 16) : (s + 1) * (HALF_S // 16)]
             nc.vector.tensor_copy(out=v_w[a, s][:], in_=tab_w[a][:].indirect(cols))
 
-        def cast_w1(a, c):
-            dst = w1_bf[a][:].rearrange("p (t m j) -> p m t j", t=PACK, j=PACK)
+        def cast_w1(a, c, on_vector=0):
             m_count = HALF_C // PACK
-            nc.scalar.copy(
-                out=dst[:, c * m_count : (c + 1) * m_count],
-                in_=w1_raw[a][c][:].rearrange("p j (m t) -> p m t j", t=PACK),
-            )
+            dst = w1_bf[a][:].rearrange("p (t m j) -> p m j t", t=PACK, j=PACK)[:, c * m_count : (c + 1) * m_count]
+            src = w1_raw[a][c][:].rearrange("p j (m t) -> p m j t", t=PACK)
+            nc.scalar.copy(out=dst[:, on_vector:], in_=src[:, on_vector:])
+            if on_vector:
+                nc.vector.tensor_copy(out=dst[:, :on_vector], in_=src[:, :on_vector])
 
         def quantize_w1(a):
             nc.vector.quantize_mx(out=w1_q[a][:].bitcast(FP8X4), scales=w1_sc[a][:], in_=w1_bf[a][:])
@@ -102,60 +99,62 @@ def tile_list_cane_blade_pairing_kernel(
         def deal_w2(a):
             nc.vector.tensor_copy(
                 out=w2_q[a][:].rearrange("p (t g i) -> p g t i", t=PACK, i=4),
-                in_=w2_raw[a][:].rearrange("p (g i t) -> p g t i", t=PACK, i=4),
+                in_=w2_raw[:, a, :].rearrange("p (g i t) -> p g t i", t=PACK, i=4),
             )
 
         gather_words(0, 0)
         gather_words(0, 1)
         nc.vector.tensor_copy(out=v_sc[0][:], in_=tab_sc[:].indirect(offs_t[:]))
-        for a in range(1, PASSES):
-            for u in range(2):
-                first = 4 * (2 * a + u - 1)
-                nc.gpsimd.dma_start(
-                    out=v_sc[a][:].bitcast(I32)[64 * u : 64 * u + 64, :],
-                    in_=v_sc[0][:].bitcast(I32)[first : first + 64, :],
-                )
-        load_w1(0, 0)
-        load_w1(0, 1)
+        nc.sync.dma_start(out=w2_raw[:], in_=w2_words.rearrange("a p c i -> p a (c i)").bitcast(I32))
         load_tab(1)
         w2_sc_words = w2_sc_raw[:].bitcast(I32).rearrange("p (a c) -> p a c", a=PASSES)
         w2_sc_rows = w2_scales.bitcast(I32).rearrange("a r c -> r a c")
         for q in range(4):
             nc.sync.dma_start(out=w2_sc_words[32 * q : 32 * q + 4], in_=w2_sc_rows[4 * q : 4 * q + 4])
-        for a in range(PASSES):
-            load_w2(a)
-        for a in range(1, PASSES):
-            load_w1(a, 0)
-            load_w1(a, 1)
+        load_w1(0, 0)
         load_tab(2)
+        load_w1(0, 1)
+        for a in range(1, PASSES):
+            v_sc.append(sb([P, S], U8, "v_sc%d" % a))
+            for u in range(2):
+                first = 4 * (2 * a + u - 1)
+                nc.sync.dma_start(
+                    out=v_sc[a][:].bitcast(I32)[64 * u : 64 * u + 64, :],
+                    in_=v_sc[0][:].bitcast(I32)[first : first + 64, :],
+                )
+        b1_t = sb([P, PACK], F32, "b1_t")
+        nc.sync.dma_start(out=b1_t[:], in_=b1.rearrange("(p t) -> p t", t=PACK))
+        load_w1(1, 0)
+        load_w1(1, 1)
+        load_w1(2, 0)
+        load_w1(2, 1)
+        gain_t = sb([P, PACK], F32, "gain_t")
         nc.sync.dma_start(pos2_t[:], pos2)
         nc.sync.dma_start(pos1_t[:], pos1)
-
-        b1_t = sb([P, PACK], F32, "b1_t")
-        gain_t = sb([P, PACK], F32, "gain_t")
-        nc.sync.dma_start(out=b1_t[:], in_=b1.rearrange("(p t) -> p t", t=PACK))
         nc.sync.dma_start(out=gain_t[:], in_=gain.rearrange("(p t) -> p t", t=PACK))
-
         for q in range(4):
             nc.sync.dma_start(
                 out=w4_sc[:].bitcast(I32)[32 * q : 32 * q + 4, :], in_=w4_scales[0].bitcast(I32)[4 * q : 4 * q + 4, :]
             )
-        for a in range(PASSES):
-            cast_w1(a, 0)
-            cast_w1(a, 1)
-        gather_words(1, 0)
-        gather_words(1, 1)
-        quantize_w1(0)
+        cast_w1(0, 0)
+        cast_w1(0, 1)
+        cast_w1(1, 0)
+        cast_w1(1, 1)
+        cast_w1(2, 0)
         nc.vector.tensor_copy(
             out=w2_sc[:].rearrange("p (a t m) -> p a t m", a=PASSES, t=PACK),
             in_=w2_sc_raw[:].rearrange("p (a m t) -> p a t m", a=PASSES, t=PACK),
         )
         for a in range(PASSES):
             deal_w2(a)
-        quantize_w1(1)
+        gather_words(1, 0)
+        gather_words(1, 1)
         gather_words(2, 0)
+        quantize_w1(0)
+        gather_words(2, 1, tag="w1_bf0")
+        quantize_w1(1)
+        cast_w1(2, 1, on_vector=40)
         quantize_w1(2)
-        gather_words(2, 1, tag="w1_bf2")
 
         w4_w = sb([P, 2 * N], U8, "w4_w")
         nc.sync.dma_start(out=w4_w[:].bitcast(I32), in_=w4_words[0].bitcast(I32))
@@ -185,17 +184,19 @@ def tile_list_cane_blade_pairing_kernel(
                 )
             return bank
 
+        first_sizes = sb([P, 4, HALF_S], F32, "first_sizes", tag="w1_bf2")
+
         def first_stage(t):
             for s in range(2):
                 warp = product(t, s, 0, w2_q, lambda a: w2_sc[:, a * H + t * P : a * H + (t + 1) * P])
                 lift = product(t, s, 1, w1_q, lambda a: w1_sc[a][:, t * P : (t + 1) * P])
-                size = sb([P, HALF_S], F32, "size%d%d" % (t, s))
-                nc.scalar.activation(out=size[:], in_=warp[:], func=ACT.Abs)
+                size = first_sizes[:, 2 * t + s, :] if t < 2 else sb([P, HALF_S], F32, "size%d%d" % (t, s))[:]
+                nc.scalar.activation(out=size, in_=warp[:], func=ACT.Abs)
                 nc.vector.scalar_tensor_tensor(
                     out=h[t][:, s * HALF_S : (s + 1) * HALF_S],
                     in0=lift[:],
                     scalar=b1_t[:, t : t + 1],
-                    in1=size[:],
+                    in1=size,
                     op0=ALU.add,
                     op1=ALU.subtract,
                 )
@@ -240,22 +241,23 @@ def tile_list_cane_blade_pairing_kernel(
                         start=True,
                         stop=True,
                     )
-                capped = sb([P, 2, HALF_J], F32, "capped%d%d" % (g, i))
-                nc.vector.tensor_tensor(
-                    out=capped[:],
-                    in0=bank[:].rearrange("p (u j) -> p u j", u=2),
-                    in1=caps_t[i][:, :, j_cols],
-                    op=ALU.min,
-                )
-                nc.sync.dma_start(
-                    out=out[2 * i * P : 2 * (i + 1) * P, j_cols].rearrange("(u p) j -> p u j", p=P), in_=capped[:]
-                )
+                pieces = [(0, 1), (1, 2)] if (g, i) == (1, N_TILES // 2 - 1) else [(0, 2)]
+                for u0, u1 in pieces:
+                    capped = sb([P, u1 - u0, HALF_J], F32, "capped%d%d%d" % (g, i, u0))
+                    nc.vector.tensor_tensor(
+                        out=capped[:],
+                        in0=bank[:].rearrange("p (u j) -> p u j", u=2)[:, u0:u1],
+                        in1=caps_t[i][:, u0:u1, j_cols],
+                        op=ALU.min,
+                    )
+                    rows = out[(2 * i + u0) * P : (2 * i + u1) * P, j_cols]
+                    nc.sync.dma_start(out=rows.rearrange("(u p) j -> p u j", p=P), in_=capped[:])
 
         last = PACK - 1
         for t in range(PACK):
             first_stage(t)
             if t > 0:
-                sine(t - 1, tag="size%d1" % t)
+                sine(t - 1, tag="w1_bf2" if t == 1 else "size%d1" % t)
             lower_blade(t)
         sine(last)
         early = sb([P, PACK, HALF_J], F32, "early_totals", tag="lower%d" % (last - 1))

@@ -52,7 +52,11 @@ def tile_list_cane_blade_pairing_kernel(
         pos1_t = keep.tile([P, PAIRS // 16], U16, name="pos1_t")
         pos2_t = keep.tile([P, PAIRS // 16], U16, name="pos2_t")
         tab_w = [sb([P, T], U16, "tab_w%d" % a) for a in range(PASSES)]
-        w1_raw = [[sb([P, PACK, HALF_C], F32, "w1_raw%d%d" % (a, c)) for c in range(2)] for a in range(PASSES)]
+        w1_first = sb([P, PACK, H], F32, "w1_first")
+        w1_raw = {(0, c): w1_first[:, :, c * HALF_C : (c + 1) * HALF_C] for c in range(2)}
+        for a in range(1, PASSES):
+            for c in range(2):
+                w1_raw[a, c] = sb([P, PACK, HALF_C], F32, "w1_raw%d%d" % (a, c))[:]
         w2_raw = sb([P, PASSES, H], I32, "w2_raw")
 
         def load_tab(a):
@@ -60,7 +64,7 @@ def tile_list_cane_blade_pairing_kernel(
 
         def load_w1(a, c):
             rows = w1[a * P * PACK : (a + 1) * P * PACK, c * HALF_C : (c + 1) * HALF_C]
-            nc.sync.dma_start(out=w1_raw[a][c][:], in_=rows.rearrange("(p j) c -> p j c", j=PACK))
+            nc.sync.dma_start(out=w1_raw[a, c], in_=rows.rearrange("(p j) c -> p j c", j=PACK))
 
         nc.sync.dma_start(offs_t[:], offs)
         load_tab(0)
@@ -88,7 +92,7 @@ def tile_list_cane_blade_pairing_kernel(
         def cast_w1(a, c, on_vector=0):
             m_count = HALF_C // PACK
             dst = w1_bf[a][:].rearrange("p (t m j) -> p m j t", t=PACK, j=PACK)[:, c * m_count : (c + 1) * m_count]
-            src = w1_raw[a][c][:].rearrange("p j (m t) -> p m j t", t=PACK)
+            src = w1_raw[a, c].rearrange("p j (m t) -> p m j t", t=PACK)
             nc.scalar.copy(out=dst[:, on_vector:], in_=src[:, on_vector:])
             if on_vector:
                 nc.vector.tensor_copy(out=dst[:, :on_vector], in_=src[:, :on_vector])
@@ -98,22 +102,21 @@ def tile_list_cane_blade_pairing_kernel(
 
         def deal_w2(a):
             nc.vector.tensor_copy(
-                out=w2_q[a][:].rearrange("p (t g i) -> p g t i", t=PACK, i=4),
-                in_=w2_raw[:, a, :].rearrange("p (g i t) -> p g t i", t=PACK, i=4),
+                out=w2_q[a][:].rearrange("p (t m) -> p m t", t=PACK),
+                in_=w2_raw[:, a, :].rearrange("p (m t) -> p m t", t=PACK),
             )
 
         gather_words(0, 0)
         gather_words(0, 1)
         nc.vector.tensor_copy(out=v_sc[0][:], in_=tab_sc[:].indirect(offs_t[:]))
         nc.sync.dma_start(out=w2_raw[:], in_=w2_words.rearrange("a p c i -> p a (c i)").bitcast(I32))
-        load_tab(1)
         w2_sc_words = w2_sc_raw[:].bitcast(I32).rearrange("p (a c) -> p a c", a=PASSES)
         w2_sc_rows = w2_scales.bitcast(I32).rearrange("a r c -> r a c")
         for q in range(4):
             nc.sync.dma_start(out=w2_sc_words[32 * q : 32 * q + 4], in_=w2_sc_rows[4 * q : 4 * q + 4])
-        load_w1(0, 0)
+        load_tab(1)
+        nc.sync.dma_start(out=w1_first[:], in_=w1[0 : P * PACK, :].rearrange("(p j) c -> p j c", j=PACK))
         load_tab(2)
-        load_w1(0, 1)
         for a in range(1, PASSES):
             v_sc.append(sb([P, S], U8, "v_sc%d" % a))
             for u in range(2):
@@ -142,8 +145,8 @@ def tile_list_cane_blade_pairing_kernel(
         cast_w1(1, 1)
         cast_w1(2, 0)
         nc.vector.tensor_copy(
-            out=w2_sc[:].rearrange("p (a t m) -> p a t m", a=PASSES, t=PACK),
-            in_=w2_sc_raw[:].rearrange("p (a m t) -> p a t m", a=PASSES, t=PACK),
+            out=w2_sc[:].rearrange("p (a t m) -> p t a m", a=PASSES, t=PACK),
+            in_=w2_sc_raw[:].rearrange("p (a m t) -> p t a m", a=PASSES, t=PACK),
         )
         for a in range(PASSES):
             deal_w2(a)
@@ -226,9 +229,9 @@ def tile_list_cane_blade_pairing_kernel(
         def quantize_z(g):
             nc.vector.quantize_mx(out=z_q[g][:].bitcast(FP8X4), scales=z_sc[g][:], in_=z_bf[g][:])
 
-        def scores(g):
+        def scores(g, pairs_of_tiles, tag=""):
             j_cols = slice(g * HALF_J, (g + 1) * HALF_J)
-            for i in range(N_TILES // 2):
+            for i in pairs_of_tiles:
                 bank = psum.tile([P, 2 * HALF_J], F32, name="bank", tag="bank%d" % (3 * g + i))
                 for u in range(2):
                     n0 = (2 * i + u) * P
@@ -243,7 +246,7 @@ def tile_list_cane_blade_pairing_kernel(
                     )
                 pieces = [(0, 1), (1, 2)] if (g, i) == (1, N_TILES // 2 - 1) else [(0, 2)]
                 for u0, u1 in pieces:
-                    capped = sb([P, u1 - u0, HALF_J], F32, "capped%d%d%d" % (g, i, u0))
+                    capped = sb([P, u1 - u0, HALF_J], F32, "capped%d%d%d" % (g, i, u0), tag=tag)
                     nc.vector.tensor_tensor(
                         out=capped[:],
                         in0=bank[:].rearrange("p (u j) -> p u j", u=2)[:, u0:u1],
@@ -269,6 +272,7 @@ def tile_list_cane_blade_pairing_kernel(
         quantize_z(0)
         upper_blade(2, 1, late[:, 2, :])
         upper_blade(3, 1, late[:, 3, :])
-        scores(0)
+        scores(0, range(2))
         quantize_z(1)
-        scores(1)
+        scores(0, [2], tag="z_bf1")
+        scores(1, range(N_TILES // 2))

from contextlib import ExitStack

import concourse.mybir as mybir

K, T, S, H, PAIRS, N = 1536, 2048, 1024, 512, 512, 768
FLOPS = 2 * (2 * K * H * S + H * N * PAIRS)

F32 = mybir.dt.float32
BF16 = mybir.dt.bfloat16
I32 = mybir.dt.int32
U32 = mybir.dt.uint32
U16 = mybir.dt.uint16
U8 = mybir.dt.uint8
FP8X4 = mybir.dt.float8_e4m3fn_x4
FP4X4 = mybir.dt.float4_e2m1fn_x4
ACT = mybir.ActivationFunctionType
ALU = mybir.AluOpType

P = 128
PACK = 4
PASSES = K // (P * PACK)
HALF_S = S // 2
HALF_J = PAIRS // 2
HALF_C = H // 2
N_TILES = N // P
ALIGN = 64


def tile_list_cane_blade_pairing_kernel(
    tc, tab_words, tab_scales, offs, pos1, pos2, w1, w2_words, w2_scales, b1, gain, w4_words, w4_scales, caps, out
):
    nc = tc.nc
    with ExitStack() as ctx:
        keep = ctx.enter_context(tc.tile_pool(name="keep", bufs=1))
        psum = ctx.enter_context(tc.psum_pool(name="psum", bufs=1))

        def sb(shape, dtype, name, tag=""):
            return keep.tile(shape, dtype, name=name, tag=tag or name, align_bytes=ALIGN)

        tab_sc = sb([P, T], U8, "tab_sc")
        w2_sc_raw = sb([P, PASSES * H], U8, "w2_sc_raw")
        w4_sc = sb([P, N], U8, "w4_sc")
        warm = sb([P, 2], F32, "warm")
        nc.gpsimd.memset(tab_sc[:].bitcast(I32), 0)
        nc.vector.memset(w2_sc_raw[:].bitcast(I32), 0)
        nc.vector.memset(w4_sc[:].bitcast(I32), 0)
        nc.vector.memset(warm[:, 0:1], 0.0)
        warm_out = sb([P, 1], F32, "warm_out")
        nc.scalar.activation(out=warm_out[:], in_=warm[:, 0:1], func=ACT.Sin)

        offs_t = keep.tile([P, S // 16], U16, name="offs_t")
        pos1_t = keep.tile([P, PAIRS // 16], U16, name="pos1_t")
        pos2_t = keep.tile([P, PAIRS // 16], U16, name="pos2_t")
        tab_w = [sb([P, T], U16, "tab_w%d" % a) for a in range(PASSES)]
        w1_first = sb([P, PACK, H], F32, "w1_first")
        w1_raw = {(0, c): w1_first[:, :, c * HALF_C : (c + 1) * HALF_C] for c in range(2)}
        for a in range(1, PASSES):
            for c in range(2):
                w1_raw[a, c] = sb([P, PACK, HALF_C], F32, "w1_raw%d%d" % (a, c))[:]
        w2_raw = sb([P, PASSES, H], I32, "w2_raw")

        def load_tab(a):
            nc.sync.dma_start(out=tab_w[a][:].bitcast(I32), in_=tab_words[a].bitcast(I32))

        def load_w1(a, c):
            rows = w1[a * P * PACK : (a + 1) * P * PACK, c * HALF_C : (c + 1) * HALF_C]
            nc.sync.dma_start(out=w1_raw[a, c], in_=rows.rearrange("(p j) c -> p j c", j=PACK))

        nc.sync.dma_start(offs_t[:], offs)
        load_tab(0)
        tab_sc_words = tab_sc[:].bitcast(I32)
        scale_rows = tab_scales.bitcast(I32).rearrange("a (u e r) t -> e (a u) r t", u=2, e=2)
        for e in range(2):
            nc.sync.dma_start(out=tab_sc_words[32 * e + 4 : 32 * e + 20, :], in_=scale_rows[e, 2:6])
        for u in range(2):
            for e in range(2):
                q = 2 * u + e
                nc.sync.dma_start(out=tab_sc_words[32 * q : 32 * q + 4, :], in_=scale_rows[e, u])
        v_w = {}
        v_sc = [sb([P, S], U8, "v_sc0")]
        w1_bf = [sb([P, H * PACK], BF16, "w1_bf%d" % a) for a in range(PASSES)]
        w1_q = [sb([P, H], U32, "w1_q%d" % a) for a in range(PASSES)]
        w1_sc = [sb([P, H], U8, "w1_sc%d" % a) for a in range(PASSES)]
        w2_q = [sb([P, H], I32, "w2_q%d" % a) for a in range(PASSES)]
        w2_sc = sb([P, PASSES * H], U8, "w2_sc")

        def gather_words(a, s, tag=""):
            v_w[a, s] = sb([P, HALF_S], U16, "v_w%d%d" % (a, s), tag=tag)
            cols = offs_t[:, s * (HALF_S // 16) : (s + 1) * (HALF_S // 16)]
            nc.vector.tensor_copy(out=v_w[a, s][:], in_=tab_w[a][:].indirect(cols))

        def cast_w1(a, c, on_vector=0):
            m_count = HALF_C // PACK
            dst = w1_bf[a][:].rearrange("p (t m j) -> p m j t", t=PACK, j=PACK)[:, c * m_count : (c + 1) * m_count]
            src = w1_raw[a, c].rearrange("p j (m t) -> p m j t", t=PACK)
            nc.scalar.copy(out=dst[:, on_vector:], in_=src[:, on_vector:])
            if on_vector:
                nc.vector.tensor_copy(out=dst[:, :on_vector], in_=src[:, :on_vector])

        def quantize_w1(a):
            nc.vector.quantize_mx(out=w1_q[a][:].bitcast(FP8X4), scales=w1_sc[a][:], in_=w1_bf[a][:])

        def deal_w2(a):
            nc.vector.tensor_copy(
                out=w2_q[a][:].rearrange("p (t m) -> p m t", t=PACK),
                in_=w2_raw[:, a, :].rearrange("p (m t) -> p m t", t=PACK),
            )

        gather_words(0, 0)
        gather_words(0, 1)
        nc.vector.tensor_copy(out=v_sc[0][:], in_=tab_sc[:].indirect(offs_t[:]))
        nc.sync.dma_start(out=w2_raw[:], in_=w2_words.rearrange("a p c i -> p a (c i)").bitcast(I32))
        w2_sc_words = w2_sc_raw[:].bitcast(I32).rearrange("p (a c) -> p a c", a=PASSES)
        w2_sc_rows = w2_scales.bitcast(I32).rearrange("a r c -> r a c")
        for q in range(4):
            nc.sync.dma_start(out=w2_sc_words[32 * q : 32 * q + 4], in_=w2_sc_rows[4 * q : 4 * q + 4])
        load_tab(1)
        nc.sync.dma_start(out=w1_first[:], in_=w1[0 : P * PACK, :].rearrange("(p j) c -> p j c", j=PACK))
        load_tab(2)
        for a in range(1, PASSES):
            v_sc.append(sb([P, S], U8, "v_sc%d" % a))
            for u in range(2):
                first = 4 * (2 * a + u - 1)
                nc.sync.dma_start(
                    out=v_sc[a][:].bitcast(I32)[64 * u : 64 * u + 64, :],
                    in_=v_sc[0][:].bitcast(I32)[first : first + 64, :],
                )
        b1_t = sb([P, PACK], F32, "b1_t")
        nc.sync.dma_start(out=b1_t[:], in_=b1.rearrange("(p t) -> p t", t=PACK))
        load_w1(1, 0)
        load_w1(1, 1)
        load_w1(2, 0)
        load_w1(2, 1)
        gain_t = sb([P, PACK], F32, "gain_t")
        nc.sync.dma_start(pos2_t[:], pos2)
        nc.sync.dma_start(pos1_t[:], pos1)
        nc.sync.dma_start(out=gain_t[:], in_=gain.rearrange("(p t) -> p t", t=PACK))
        for q in range(4):
            nc.sync.dma_start(
                out=w4_sc[:].bitcast(I32)[32 * q : 32 * q + 4, :], in_=w4_scales[0].bitcast(I32)[4 * q : 4 * q + 4, :]
            )
        cast_w1(0, 0)
        cast_w1(0, 1)
        cast_w1(1, 0)
        cast_w1(1, 1)
        cast_w1(2, 0)
        nc.vector.tensor_copy(
            out=w2_sc[:].rearrange("p (a t m) -> p t a m", a=PASSES, t=PACK),
            in_=w2_sc_raw[:].rearrange("p (a m t) -> p t a m", a=PASSES, t=PACK),
        )
        for a in range(PASSES):
            deal_w2(a)
        gather_words(1, 0)
        gather_words(1, 1)
        gather_words(2, 0)
        quantize_w1(0)
        gather_words(2, 1, tag="w1_bf0")
        quantize_w1(1)
        cast_w1(2, 1, on_vector=40)
        quantize_w1(2)

        w4_w = sb([P, 2 * N], U8, "w4_w")
        nc.sync.dma_start(out=w4_w[:].bitcast(I32), in_=w4_words[0].bitcast(I32))
        spent = ["w1_raw11", "w1_raw20", "w1_raw21"]
        caps_t = [sb([P, 2, PAIRS], F32, "caps%d" % i, tag=spent[i]) for i in range(N_TILES // 2)]
        for i in range(N_TILES // 2):
            nc.sync.dma_start(
                out=caps_t[i][:], in_=caps[2 * i * P : 2 * (i + 1) * P, :].rearrange("(u p) j -> p u j", p=P)
            )

        z_bf = [sb([P, HALF_J * PACK], BF16, "z_bf%d" % g) for g in range(2)]
        h = [sb([P, S], F32, "h%d" % t) for t in range(PACK)]
        sines = {}
        lowers = {}

        def product(t, s, kind, codes, scale_of):
            bank = psum.tile([P, HALF_S], F32, name="bank", tag="bank%d" % (4 * (t % 2) + 2 * s + kind))
            for a in range(PASSES):
                nc.tensor.matmul_mx(
                    out=bank[:],
                    lhsT=codes[a][:, t * P : (t + 1) * P].bitcast(FP8X4),
                    lhsT_scale=scale_of(a),
                    rhs=v_w[a, s][:].bitcast(FP4X4),
                    rhs_scale=v_sc[a][:, s * HALF_S : (s + 1) * HALF_S],
                    start=(a == 0),
                    stop=(a == PASSES - 1),
                )
            return bank

        first_sizes = sb([P, 4, HALF_S], F32, "first_sizes", tag="w1_bf2")

        def first_stage(t):
            for s in range(2):
                warp = product(t, s, 0, w2_q, lambda a: w2_sc[:, a * H + t * P : a * H + (t + 1) * P])
                lift = product(t, s, 1, w1_q, lambda a: w1_sc[a][:, t * P : (t + 1) * P])
                size = first_sizes[:, 2 * t + s, :] if t < 2 else sb([P, HALF_S], F32, "size%d%d" % (t, s))[:]
                nc.scalar.activation(out=size, in_=warp[:], func=ACT.Abs)
                nc.vector.scalar_tensor_tensor(
                    out=h[t][:, s * HALF_S : (s + 1) * HALF_S],
                    in0=lift[:],
                    scalar=b1_t[:, t : t + 1],
                    in1=size,
                    op0=ALU.add,
                    op1=ALU.subtract,
                )

        def lower_blade(t):
            lower = sb([P, PAIRS], F32, "lower%d" % t)
            nc.vector.tensor_copy(out=lower[:], in_=h[t][:].indirect(pos2_t[:]))
            lowers[t] = lower

        def sine(t, tag=""):
            sines[t] = sb([P, PAIRS], F32, "sine%d" % t, tag=tag)
            nc.scalar.activation(out=sines[t][:], in_=lowers[t][:], func=ACT.Sin)

        def upper_blade(t, g, total):
            cols = pos1_t[:, g * (HALF_J // 16) : (g + 1) * (HALF_J // 16)]
            nc.vector.tensor_tensor(out=total, in0=h[t][:].indirect(cols), in1=sines[t][:, g * HALF_J : (g + 1) * HALF_J], op=ALU.add)
            nc.scalar.activation(
                out=z_bf[g][:].rearrange("p (j t) -> p t j", t=PACK)[:, t, :],
                in_=total,
                func=ACT.Copy,
                scale=gain_t[:, t : t + 1],
            )

        z_q = [sb([P, HALF_J], U32, "z_q%d" % g) for g in range(2)]
        z_sc = [sb([P, HALF_J], U8, "z_sc%d" % g) for g in range(2)]

        def quantize_z(g):
            nc.vector.quantize_mx(out=z_q[g][:].bitcast(FP8X4), scales=z_sc[g][:], in_=z_bf[g][:])

        def scores(g, pairs_of_tiles, tag=""):
            j_cols = slice(g * HALF_J, (g + 1) * HALF_J)
            for i in pairs_of_tiles:
                bank = psum.tile([P, 2 * HALF_J], F32, name="bank", tag="bank%d" % (3 * g + i))
                for u in range(2):
                    n0 = (2 * i + u) * P
                    nc.tensor.matmul_mx(
                        out=bank[:, u * HALF_J : (u + 1) * HALF_J],
                        lhsT=w4_w[:, 2 * n0 : 2 * (n0 + P)].bitcast(FP4X4),
                        lhsT_scale=w4_sc[:, n0 : n0 + P],
                        rhs=z_q[g][:].bitcast(FP8X4),
                        rhs_scale=z_sc[g][:],
                        start=True,
                        stop=True,
                    )
                pieces = [(0, 1), (1, 2)] if (g, i) == (1, N_TILES // 2 - 1) else [(0, 2)]
                for u0, u1 in pieces:
                    capped = sb([P, u1 - u0, HALF_J], F32, "capped%d%d%d" % (g, i, u0), tag=tag)
                    nc.vector.tensor_tensor(
                        out=capped[:],
                        in0=bank[:].rearrange("p (u j) -> p u j", u=2)[:, u0:u1],
                        in1=caps_t[i][:, u0:u1, j_cols],
                        op=ALU.min,
                    )
                    rows = out[(2 * i + u0) * P : (2 * i + u1) * P, j_cols]
                    nc.sync.dma_start(out=rows.rearrange("(u p) j -> p u j", p=P), in_=capped[:])

        last = PACK - 1
        for t in range(PACK):
            first_stage(t)
            if t > 0:
                sine(t - 1, tag="w1_bf2" if t == 1 else "size%d1" % t)
            lower_blade(t)
        sine(last)
        early = sb([P, PACK, HALF_J], F32, "early_totals", tag="lower%d" % (last - 1))
        for t in range(PACK):
            upper_blade(t, 0, early[:, t, :])
        late = sb([P, PACK, HALF_J], F32, "late_totals", tag="lower%d" % last)
        upper_blade(0, 1, late[:, 0, :])
        upper_blade(1, 1, late[:, 1, :])
        quantize_z(0)
        upper_blade(2, 1, late[:, 2, :])
        upper_blade(3, 1, late[:, 3, :])
        scores(0, range(2))
        quantize_z(1)
        scores(0, [2], tag="z_bf1")
        scores(1, range(N_TILES // 2))
